import numpy as np, ml_dtypes
CORES = [50,52,122,124]
N = 4
import mx_ref
NC = 128
C2 = np.float32(0.304)
BF = ml_dtypes.bfloat16
def cut(t, i, w=512):
    return t[:, w * i:w * i + w]
def tile(rs):
    return np.stack(rs, axis=2).reshape(128, -1).astype(BF)
def pick(b):
    s = np.zeros((128, 128, 4), np.float32)
    s[np.arange(128), np.arange(128), b] = 1.0
    return mx_ref.quantize(s.reshape(128, 512).astype(BF))
def setup_inputs(rng):
    def f(*shape):
        return mx_ref.flush((rng.standard_normal(shape, dtype=np.float32) * np.exp2(rng.integers(-2, 3, shape[:-1] + (1,)))).astype(BF))
    return {"b": f(N, 128, N * 512), "x": f(N, 128, 4 * NC)}
def setup_inputs_blocks(rng):
    d = setup_inputs(rng)
    for k in ("b", "x"): d[k] = mx_ref.spread(d[k], rng, 2)
    return d
def setup_inputs_wide(rng):
    d = setup_inputs(rng)
    for k in ("b", "x"): d[k] = mx_ref.flush((d[k].astype(np.float32) * np.exp2(rng.integers(-4, 5, (N, 1, 1))).astype(np.float32)).astype(BF))
    return d
def reference(b, x, own=None):
    S = [pick(t) for t in range(4)]
    h = np.zeros((N, 128, 512), BF)
    for c in range(N):
        for r in range(N):
            q = mx_ref.quantize(cut(b[r], c))
            P = [mx_ref.matmul(S[t], q) for t in range(4)]
            Z = P if r == 0 else [z + p for z, p in zip(Z, P)]
        h[c] = tile([np.maximum(Z[t], 0) * C2 for t in range(4)])
    use = h if own is None else own["h"]
    H = [mx_ref.quantize(use[j]) for j in range(N)]
    y = np.zeros((N, 128, N * NC), np.float32)
    for r in range(N):
        qx = mx_ref.quantize(x[r])
        for j in range(N):
            y[r][:, NC * j:NC * j + NC] = mx_ref.matmul(H[j], qx)
    return {"h": h, "y": y}

@@ -1,0 +1,209 @@
+from concourse.bass import DstId, RemoteDMATransfer
+from concourse.mybir import dt, AluOpType, ActivationFunctionType
+
+F8, U8, BF, F32 = "float8_e4m3fn_x4", "uint8", "bfloat16", "float32"
+W = 128
+E = 4 * W
+SCRATCH = {
+    "tb": ("sbuf", [128, 4 * E], BF), "tx": ("sbuf", [128, E], BF), "ones": ("sbuf", [128, E + 8], BF),
+    "th": ("sbuf", [128, E], BF), "ty": ("sbuf", [128, 4 * W], F32),
+    "qg": ("sbuf", [128, 4 * W], F8), "sg": ("sbuf", [128, 4 * W], U8),
+    "qs": ("sbuf", [128, 4 * W], F8), "ss": ("sbuf", [128, 4 * W], U8),
+    "qx": ("sbuf", [128, W], F8), "sx": ("sbuf", [128, W], U8),
+    "qh": ("sbuf", [128, W], F8), "sh": ("sbuf", [128, W], U8),
+    "lqg": ("sbuf", [128, 4 * W], F8), "lsg": ("sbuf", [128, 4 * W], U8),
+    "lqh": ("sbuf", [128, 4 * W], F8), "lsh": ("sbuf", [128, 4 * W], U8),
+    "rqg": ("sbuf", [128, W], F8), "rsg": ("sbuf", [128, 2 * W], U8),
+    "rqh": ("sbuf", [128, W], F8), "rsh": ("sbuf", [128, W], U8),
+    "z": ("psum", [128, 2048], F32), "yp": ("psum", [128, 2048], F32),
+}
+SEMAPHORES = (["lfar", "lnear", "lown", "lx", "zero", "diag", "qfar", "qnear", "qs", "qown", "qx", "hv", "hs", "qh",
+               "sentg", "senth", "stored", "relayg", "relayh"]
+              + [n + str(i) for n in ("g", "h", "z", "m", "c") for i in range(4)])
+
+
+def engines(mask):
+    return [e for e in range(mask.bit_length()) if (mask >> e) & 1]
+
+
+def share(es, i, n):
+    k = len(es) // n
+    return es[i * k:(i + 1) * k]
+
+
+def blk(i, n=1):
+    return slice(W * i, W * (i + n))
+
+
+def plan(cores, topo):
+    calls = []
+    everyone = range(topo.CHIPS * topo.CORES_PER_CHIP)
+    for r, me in enumerate(cores):
+        near = [c for c in range(4) if c != r and topo.chip(cores[c]) == topo.chip(me)]
+        far = [c for c in range(4) if topo.chip(cores[c]) != topo.chip(me)]
+        off = [cores[f] for f in far]
+        direct = all(topo.may_write(me, f) for f in off)
+        helpers = [c for c in everyone if c not in cores and topo.chip(c) == topo.chip(me)
+                   and all(topo.may_write(c, f) for f in off)]
+        helpers.sort(key=lambda c: (topo.die(c) != topo.die(me), c))
+        coders, scaler = helpers[:len(far)], helpers[len(far)]
+        for ph in ("g", "h"):
+            def src(kind, c, n=1):
+                return (kind + ph, blk(c, n) if ph == "g" else blk(0))
+
+            def land(kind):
+                return ("l" + kind + ph, blk(r))
+            sem = ph + str(r)
+            q_far, q_near = (["qfar"], ["qnear"]) if ph == "g" else (["qh"], [])
+            if direct:
+                out = engines(topo.mask(me, off[0]))
+                inn = [e for e in engines(topo.mask(me, cores[near[0]])) if e not in out]
+                for kind in ("q", "s"):
+                    items = [(cores[f], sem, share(out, i, len(far)), kind, src(kind, f), land(kind))
+                             for i, f in enumerate(far)]
+                    items += [(cores[c], sem, share(inn, i, len(near)), kind, src(kind, c), land(kind))
+                              for i, c in enumerate(near)]
+                    calls.append(dict(core=me, ph=ph, needs=q_far + q_near, items=items))
+                continue
+            wide = len(far) if ph == "g" else 1
+            calls.append(dict(core=me, ph=ph, needs=q_far, items=[
+                (scaler, "relay" + ph, engines(topo.mask(me, scaler)), "s", src("s", far[0], wide),
+                 ("rs" + ph, blk(0, wide)))]))
+            calls.append(dict(core=me, ph=ph, needs=q_far, items=[
+                (h, "relay" + ph, share(engines(topo.mask(me, h)), i, len(far)), "q", src("q", f), ("rq" + ph, blk(0)))
+                for i, (h, f) in enumerate(zip(coders, far))]))
+            for kind in ("q", "s"):
+                calls.append(dict(core=me, ph=ph, needs=q_near, items=[
+                    (cores[c], sem, share(engines(topo.mask(me, cores[c])), i, len(near)), kind, src(kind, c), land(kind))
+                    for i, c in enumerate(near)]))
+            calls.append(dict(core=scaler, ph=ph, needs=["relay" + ph], items=[
+                (cores[f], sem, share(engines(topo.mask(scaler, cores[f])), i, len(far)), "s",
+                 ("rs" + ph, blk(i if ph == "g" else 0)), land("s")) for i, f in enumerate(far)]))
+            for h, f in zip(coders, far):
+                calls.append(dict(core=h, ph=ph, needs=["relay" + ph], items=[
+                    (cores[f], sem, engines(topo.mask(h, cores[f])), "q", ("rq" + ph, blk(0)), land("q"))]))
+    return calls
+
+
+def rank_program(g, core, T, topo):
+    calls = plan(T.cores, topo)
+    got = {}
+    for c in calls:
+        for dst, sem, es, *_ in c["items"]:
+            if dst == core:
+                got[sem] = got.get(sem, 0) + len(es)
+
+    def view(kind, where):
+        ap = T[where[0]][:, where[1]]
+        return ap.bitcast(dt.uint8) if kind == "q" else ap
+
+    def send(ph):
+        total, seen = 0, []
+        for c in calls:
+            if c["core"] != core or c["ph"] != ph:
+                continue
+            for n in c["needs"]:
+                if n not in seen:
+                    seen.append(n)
+                    g.wait_ge(T.sem[n], got.get(n, 1))
+            ts = []
+            for dst, sem, es, kind, s, d in c["items"]:
+                rid, pid, _ = topo.addr(dst)
+                ts.append(RemoteDMATransfer(dst_ids=[DstId(rid=rid, pnc=pid)], dma_engine_mask=sum(1 << e for e in es),
+                                            remote_sem=T.sem[sem], src=view(kind, s), dst=view(kind, d)))
+                total += len(es)
+            g.remote_dma_fused(ts, local_sem=T.sem["sent" + ph])
+        return total
+
+    rank = T.rank_of(core)
+    if rank is None:
+        for ph in ("g", "h"):
+            n = send(ph)
+            if n:
+                g.wait_ge(T.sem["sent" + ph], n)
+        return
+
+    cores = T.cores
+    near = [c for c in range(4) if c != rank and topo.chip(cores[c]) == topo.chip(core)]
+    far = [c for c in range(4) if topo.chip(cores[c]) != topo.chip(core)]
+    order = near + sorted(far, key=lambda c: not topo.may_write(cores[c], core))
+    sem, v, a, t, sy = T.sem, g.vector, g.scalar, g.tensor, g.sync
+
+    lo, nf = far[0], len(far)
+    sy.dma_start(T.tb[:, E * lo:E * (lo + nf)], T.b[:, E * lo:E * (lo + nf)]).then_inc(sem.lfar, 16)
+    for name, c in (("lnear", near[0]), ("lown", rank)):
+        sy.dma_start(T.tb[:, E * c:E * c + E], T.b[:, E * c:E * c + E]).then_inc(sem[name], 16)
+    sy.dma_start(T.tx[:], T.x[:]).then_inc(sem.lx, 16)
+
+    v.memset(T.ones[:], 0.0).then_inc(sem.zero, 1)
+    g.wait_ge(sem.zero, 1)
+    diag = T.ones[:, 3:3 + E:4]
+    g.affine_select(diag, diag, [[-1, W]], AluOpType.not_equal, 1.0, 0, 1).then_inc(sem.diag, 1)
+
+    def quant_b(c, n, done):
+        v.quantize_mx(T.qg[:, blk(c, n)], T.sg[:, blk(c, n)], T.tb[:, E * c:E * (c + n)]).then_inc(done, 1)
+    v.wait_ge(sem.lfar, 16)
+    quant_b(lo, nf, sem.qfar)
+    v.wait_ge(sem.lnear, 16)
+    quant_b(near[0], 1, sem.qnear)
+    v.wait_ge(sem.diag, 1)
+    for b in range(4):
+        v.quantize_mx(T.qs[:, blk(b)], T.ss[:, blk(b)], T.ones[:, 3 - b:3 - b + E]).then_inc(sem.qs, 1)
+    v.wait_ge(sem.lown, 16)
+    quant_b(rank, 1, sem.qown)
+    v.wait_ge(sem.lx, 16)
+    v.quantize_mx(T.qx[:], T.sx[:], T.tx[:]).then_inc(sem.qx, 1)
+
+    n = send("g")
+    g.wait_ge(sem.sentg, n)
+
+    t.wait_ge(sem.qs, 4)
+    t.wait_ge(sem.qown, 1)
+    for i, c in enumerate([rank] + order):
+        q, s = (T.qg, T.sg) if c == rank else (T.lqg, T.lsg)
+        if c != rank:
+            t.wait_ge(sem["g%d" % c], got["g%d" % c])
+        for b in range(4):
+            m = t.matmul_mx(T.z[:, 512 * b:512 * b + W], T.qs[:, blk(b)], T.ss[:, blk(b)], q[:, blk(c)], s[:, blk(c)],
+                            i == 0, i == 3)
+            if i == 3:
+                m.then_inc(sem["z%d" % b], 1)
+
+    for b in range(4):
+        out, z = T.th[:, b:E:4], T.z[:, 512 * b:512 * b + W]
+        if b % 2 == 0:
+            a.wait_ge(sem["z%d" % b], 1)
+            a.activation(out, z, ActivationFunctionType.Relu, scale=0.304).then_inc(sem.hs, 1)
+        else:
+            v.wait_ge(sem["z%d" % b], 1)
+            v.tensor_scalar(out, z, 0.0, 0.304, AluOpType.max, AluOpType.mult).then_inc(sem.hv, 1)
+    v.wait_ge(sem.hs, 2)
+    v.wait_ge(sem.hv, 2)
+    v.quantize_mx(T.qh[:], T.sh[:], T.th[:]).then_inc(sem.qh, 1)
+
+    n = send("h")
+
+    sy.wait_ge(sem.hs, 2)
+    sy.wait_ge(sem.hv, 2)
+    sy.wait_ge(sem.senth, n)
+    sy.dma_start(T.h[:], T.th[:]).then_inc(sem.stored, 16)
+
+    t.wait_ge(sem.qx, 1)
+    for i, c in enumerate([rank] + order):
+        if c == rank:
+            t.wait_ge(sem.qh, 1)
+            w, ws = T.qh[:], T.sh[:]
+        else:
+            t.wait_ge(sem["h%d" % c], got["h%d" % c])
+            w, ws = T.lqh[:, blk(c)], T.lsh[:, blk(c)]
+        yp = T.yp[:, 512 * c:512 * c + W]
+        t.matmul_mx(yp, w, ws, T.qx[:], T.sx[:], True, True).then_inc(sem["m%d" % c], 1)
+        if i < 3:
+            a.wait_ge(sem["m%d" % c], 1)
+            a.activation(T.ty[:, blk(c)], yp, ActivationFunctionType.Copy).then_inc(sem["c%d" % c], 1)
+        else:
+            v.wait_ge(sem["m%d" % c], 1)
+            v.tensor_copy(T.ty[:, blk(c)], yp).then_inc(sem["c%d" % c], 1)
+        sy.wait_ge(sem["c%d" % c], 1)
+        sy.dma_start(T.y[:, blk(c)], T.ty[:, blk(c)]).then_inc(sem.stored, 16)
+    sy.wait_ge(sem.stored, 80)

@@ -17,71 +17,95 @@ SCRATCH = {
     "rqh": ("sbuf", [128, W], F8), "rsh": ("sbuf", [128, W], U8),
     "z": ("psum", [128, 2048], F32), "yp": ("psum", [128, 2048], F32),
 }
-SEMAPHORES = (["lfar", "lnear", "lown", "lx", "zero", "diag", "qfar", "qnear", "qs", "qown", "qx", "hv", "hs", "qh",
-               "sentg", "senth", "stored", "relayg", "relayh"]
-              + [n + str(i) for n in ("g", "h", "z", "m", "c") for i in range(4)])
+SEMAPHORES = (["lx", "zero", "diag", "qs", "qx", "hv", "hs", "qh", "sentg", "senth", "stored",
+               "relay0", "relay1", "relayh"]
+              + [n + str(i) for n in ("l", "q", "g", "h", "z", "m", "c") for i in range(4)])
 
 
 def engines(mask):
     return [e for e in range(mask.bit_length()) if (mask >> e) & 1]
 
 
-def share(es, i, n):
-    k = len(es) // n
-    return es[i * k:(i + 1) * k]
+def blk(i, part=None):
+    if part is None:
+        return slice(W * i, W * (i + 1))
+    return slice(W * i + W // 2 * part, W * i + W // 2 * (part + 1))
 
 
-def blk(i, n=1):
-    return slice(W * i, W * (i + n))
+def roles(r, cores, topo):
+    me = cores[r]
+    far = [c for c in range(4) if topo.chip(cores[c]) != topo.chip(me)]
+    back = [c for c in range(4) if c not in far]
+    there = topo.chip(cores[far[0]])
+
+    def crosses(c, others):
+        return all(topo.may_write(c, cores[f]) for f in others)
+
+    def idle(fits):
+        cs = [c for c in range(topo.CHIPS * topo.CORES_PER_CHIP)
+              if c not in cores and fits(topo.chip(c)) and crosses(c, far)]
+        return sorted(cs, key=lambda c: (topo.die(c) != topo.die(me), c))
+    return dict(near=[c for c in back if c != r][0], direct=crosses(me, far),
+                on_chip=idle(lambda ch: ch == topo.chip(me)),
+                at_mate=idle(lambda ch: topo.same_plane(ch, topo.chip(me)) and topo.mates(ch, there)),
+                far_direct=[f for f in far if crosses(cores[f], back)][0],
+                far_inner=[f for f in far if not crosses(cores[f], back)][0])
 
 
 def plan(cores, topo):
     calls = []
-    everyone = range(topo.CHIPS * topo.CORES_PER_CHIP)
     for r, me in enumerate(cores):
-        near = [c for c in range(4) if c != r and topo.chip(cores[c]) == topo.chip(me)]
-        far = [c for c in range(4) if topo.chip(cores[c]) != topo.chip(me)]
-        off = [cores[f] for f in far]
-        direct = all(topo.may_write(me, f) for f in off)
-        helpers = [c for c in everyone if c not in cores and topo.chip(c) == topo.chip(me)
-                   and all(topo.may_write(c, f) for f in off)]
-        helpers.sort(key=lambda c: (topo.die(c) != topo.die(me), c))
-        coders, scaler = helpers[:len(far)], helpers[len(far)]
-        for ph in ("g", "h"):
-            def src(kind, c, n=1):
-                return (kind + ph, blk(c, n) if ph == "g" else blk(0))
+        ro = roles(r, cores, topo)
+        near, fin, fdi = ro["near"], ro["far_inner"], ro["far_direct"]
 
-            def land(kind):
-                return ("l" + kind + ph, blk(r))
-            sem = ph + str(r)
-            q_far, q_near = (["qfar"], ["qnear"]) if ph == "g" else (["qh"], [])
-            if direct:
-                out = engines(topo.mask(me, off[0]))
-                inn = [e for e in engines(topo.mask(me, cores[near[0]])) if e not in out]
-                for kind in ("q", "s"):
-                    items = [(cores[f], sem, share(out, i, len(far)), kind, src(kind, f), land(kind))
-                             for i, f in enumerate(far)]
-                    items += [(cores[c], sem, share(inn, i, len(near)), kind, src(kind, c), land(kind))
-                              for i, c in enumerate(near)]
-                    calls.append(dict(core=me, ph=ph, needs=q_far + q_near, items=items))
-                continue
-            wide = len(far) if ph == "g" else 1
-            calls.append(dict(core=me, ph=ph, needs=q_far, items=[
-                (scaler, "relay" + ph, engines(topo.mask(me, scaler)), "s", src("s", far[0], wide),
-                 ("rs" + ph, blk(0, wide)))]))
-            calls.append(dict(core=me, ph=ph, needs=q_far, items=[
-                (h, "relay" + ph, share(engines(topo.mask(me, h)), i, len(far)), "q", src("q", f), ("rq" + ph, blk(0)))
-                for i, (h, f) in enumerate(zip(coders, far))]))
-            for kind in ("q", "s"):
-                calls.append(dict(core=me, ph=ph, needs=q_near, items=[
-                    (cores[c], sem, share(engines(topo.mask(me, cores[c])), i, len(near)), kind, src(kind, c), land(kind))
-                    for i, c in enumerate(near)]))
-            calls.append(dict(core=scaler, ph=ph, needs=["relay" + ph], items=[
-                (cores[f], sem, share(engines(topo.mask(scaler, cores[f])), i, len(far)), "s",
-                 ("rs" + ph, blk(i if ph == "g" else 0)), land("s")) for i, f in enumerate(far)]))
-            for h, f in zip(coders, far):
-                calls.append(dict(core=h, ph=ph, needs=["relay" + ph], items=[
-                    (cores[f], sem, engines(topo.mask(h, cores[f])), "q", ("rq" + ph, blk(0)), land("q"))]))
+        def add(core, ph, needs, *items):
+            calls.append(dict(core=core, ph=ph, needs=needs, items=items))
+
+        def to_rank(c, es, kind, ph, slot=None, part=None):
+            own = (kind + ph, blk(c if ph == "g" else 0, part))
+            where = own if slot is None else ("r" + kind + ph, blk(slot, part))
+            return (cores[c], ph + str(r), es, kind, where, ("l" + kind + ph, blk(r, part)))
+
+        def to_relay(core, sem, es, kind, ph, tile=0, slot=0, part=None):
+            return (core, sem, es, kind, (kind + ph, blk(tile, part)), ("r" + kind + ph, blk(slot, part)))
+
+        en = engines(topo.mask(me, cores[near]))
+        off = engines(topo.mask(ro["on_chip"][0], cores[fin]))
+        inn = [e for e in en if e not in off]
+        h0, h1 = off[:len(off) // 2], off[len(off) // 2:]
+        if ro["direct"]:
+            add(me, "g", ["q0"], to_rank(fin, off, "s", "g"))
+            add(me, "g", [], to_rank(fin, h0, "q", "g"))
+            add(me, "g", ["q1"], to_rank(near, inn, "s", "g"))
+            add(me, "g", ["q2"], to_rank(fdi, h1, "s", "g"))
+            add(me, "g", [], to_rank(near, inn, "q", "g"), to_rank(fdi, off, "q", "g"))
+            add(me, "h", ["qh"], to_rank(fin, h0, "s", "h"), to_rank(fdi, h1, "s", "h"))
+            add(me, "h", [], to_rank(near, inn, "q", "h"), to_rank(fin, h0, "q", "h"), to_rank(fdi, h1, "q", "h"))
+            add(me, "h", [], to_rank(near, inn, "s", "h"))
+            continue
+        a, b = ro["on_chip"][:2]
+        c = ro["on_chip"][-1]
+        d = ro["at_mate"][0]
+        add(me, "g", ["q0"], to_relay(c, "relay0", off, "s", "g", fin, 0))
+        add(me, "g", [], to_relay(b, "relay0", en, "q", "g", fin))
+        add(me, "g", ["q1"], to_relay(a, "relay1", inn, "q", "g", fdi, part=0),
+            to_relay(d, "relay1", off, "q", "g", fdi, part=1))
+        add(me, "g", [], to_relay(c, "relay1", inn, "s", "g", fdi, 1))
+        add(me, "g", ["q2"], to_rank(near, inn, "s", "g"))
+        add(me, "g", [], to_rank(near, en, "q", "g"))
+        add(c, "g", ["relay0"], to_rank(fin, off, "s", "g", 0))
+        add(b, "g", ["relay0"], to_rank(fin, off, "q", "g", 0))
+        add(a, "g", ["relay1"], to_rank(fdi, off, "q", "g", 0, part=0))
+        add(d, "g", ["relay1"], to_rank(fdi, off, "q", "g", 0, part=1))
+        add(c, "g", ["relay1"], to_rank(fdi, off, "s", "g", 1))
+        add(me, "h", ["qh"], to_relay(d, "relayh", off, "q", "h"))
+        add(me, "h", [], to_relay(b, "relayh", en, "q", "h"))
+        add(me, "h", [], to_relay(c, "relayh", inn, "s", "h"))
+        add(me, "h", [], to_rank(near, en, "s", "h"))
+        add(me, "h", [], to_rank(near, inn, "q", "h"))
+        add(d, "h", ["relayh"], to_rank(fdi, off, "q", "h", 0))
+        add(b, "h", ["relayh"], to_rank(fin, off, "q", "h", 0))
+        add(c, "h", ["relayh"], to_rank(fin, h0, "s", "h", 0), to_rank(fdi, h1, "s", "h", 0))
     return calls
 
 
@@ -89,28 +113,26 @@ def rank_program(g, core, T, topo):
     calls = plan(T.cores, topo)
     got = {}
     for c in calls:
-        for dst, sem, es, *_ in c["items"]:
+        for dst, name, es, *_ in c["items"]:
             if dst == core:
-                got[sem] = got.get(sem, 0) + len(es)
+                got[name] = got.get(name, 0) + len(es)
 
     def view(kind, where):
         ap = T[where[0]][:, where[1]]
         return ap.bitcast(dt.uint8) if kind == "q" else ap
 
     def send(ph):
-        total, seen = 0, []
+        total = 0
         for c in calls:
             if c["core"] != core or c["ph"] != ph:
                 continue
             for n in c["needs"]:
-                if n not in seen:
-                    seen.append(n)
-                    g.wait_ge(T.sem[n], got.get(n, 1))
+                g.wait_ge(T.sem[n], got.get(n, 1))
             ts = []
-            for dst, sem, es, kind, s, d in c["items"]:
+            for dst, name, es, kind, s, d in c["items"]:
                 rid, pid, _ = topo.addr(dst)
                 ts.append(RemoteDMATransfer(dst_ids=[DstId(rid=rid, pnc=pid)], dma_engine_mask=sum(1 << e for e in es),
-                                            remote_sem=T.sem[sem], src=view(kind, s), dst=view(kind, d)))
+                                            remote_sem=T.sem[name], src=view(kind, s), dst=view(kind, d)))
                 total += len(es)
             g.remote_dma_fused(ts, local_sem=T.sem["sent" + ph])
         return total
@@ -123,42 +145,35 @@ def rank_program(g, core, T, topo):
                 g.wait_ge(T.sem["sent" + ph], n)
         return
 
-    cores = T.cores
-    near = [c for c in range(4) if c != rank and topo.chip(cores[c]) == topo.chip(core)]
-    far = [c for c in range(4) if topo.chip(cores[c]) != topo.chip(core)]
-    order = near + sorted(far, key=lambda c: not topo.may_write(cores[c], core))
+    ro = roles(rank, T.cores, topo)
+    near, fin, fdi = ro["near"], ro["far_inner"], ro["far_direct"]
+    order = [near, fdi, fin]
+    leave = [fin, near, fdi] if ro["direct"] else [fin, fdi, near]
     sem, v, a, t, sy = T.sem, g.vector, g.scalar, g.tensor, g.sync
 
-    lo, nf = far[0], len(far)
-    sy.dma_start(T.tb[:, E * lo:E * (lo + nf)], T.b[:, E * lo:E * (lo + nf)]).then_inc(sem.lfar, 16)
-    for name, c in (("lnear", near[0]), ("lown", rank)):
-        sy.dma_start(T.tb[:, E * c:E * c + E], T.b[:, E * c:E * c + E]).then_inc(sem[name], 16)
-    sy.dma_start(T.tx[:], T.x[:]).then_inc(sem.lx, 16)
+    for i, c in enumerate(leave + [rank]):
+        sy.dma_start(T.tb[:, E * c:E * c + E], T.b[:, E * c:E * c + E]).then_inc(sem["l%d" % i], 16)
 
     v.memset(T.ones[:], 0.0).then_inc(sem.zero, 1)
     g.wait_ge(sem.zero, 1)
     diag = T.ones[:, 3:3 + E:4]
     g.affine_select(diag, diag, [[-1, W]], AluOpType.not_equal, 1.0, 0, 1).then_inc(sem.diag, 1)
 
-    def quant_b(c, n, done):
-        v.quantize_mx(T.qg[:, blk(c, n)], T.sg[:, blk(c, n)], T.tb[:, E * c:E * (c + n)]).then_inc(done, 1)
-    v.wait_ge(sem.lfar, 16)
-    quant_b(lo, nf, sem.qfar)
-    v.wait_ge(sem.lnear, 16)
-    quant_b(near[0], 1, sem.qnear)
-    v.wait_ge(sem.diag, 1)
-    for b in range(4):
-        v.quantize_mx(T.qs[:, blk(b)], T.ss[:, blk(b)], T.ones[:, 3 - b:3 - b + E]).then_inc(sem.qs, 1)
-    v.wait_ge(sem.lown, 16)
-    quant_b(rank, 1, sem.qown)
-    v.wait_ge(sem.lx, 16)
-    v.quantize_mx(T.qx[:], T.sx[:], T.tx[:]).then_inc(sem.qx, 1)
+    for i, c in enumerate(leave + [rank]):
+        if c == rank:
+            v.wait_ge(sem.diag, 1)
+            for b in range(4):
+                v.quantize_mx(T.qs[:, blk(b)], T.ss[:, blk(b)], T.ones[:, 3 - b:3 - b + E]).then_inc(sem.qs, 1)
+        v.wait_ge(sem["l%d" % i], 16)
+        v.quantize_mx(T.qg[:, blk(c)], T.sg[:, blk(c)], T.tb[:, E * c:E * c + E]).then_inc(sem["q%d" % i], 1)
 
     n = send("g")
     g.wait_ge(sem.sentg, n)
+    sy.wait_ge(sem.sentg, n)
+    sy.dma_start(T.tx[:], T.x[:]).then_inc(sem.lx, 16)
 
     t.wait_ge(sem.qs, 4)
-    t.wait_ge(sem.qown, 1)
+    t.wait_ge(sem.q3, 1)
     for i, c in enumerate([rank] + order):
         q, s = (T.qg, T.sg) if c == rank else (T.lqg, T.lsg)
         if c != rank:
@@ -180,6 +195,8 @@ def rank_program(g, core, T, topo):
     v.wait_ge(sem.hs, 2)
     v.wait_ge(sem.hv, 2)
     v.quantize_mx(T.qh[:], T.sh[:], T.th[:]).then_inc(sem.qh, 1)
+    v.wait_ge(sem.lx, 16)
+    v.quantize_mx(T.qx[:], T.sx[:], T.tx[:]).then_inc(sem.qx, 1)
 
     n = send("h")
 

@@ -17,8 +17,8 @@ SCRATCH = {
     "rqh": ("sbuf", [128, W], F8), "rsh": ("sbuf", [128, W], U8),
     "z": ("psum", [128, 2048], F32), "yp": ("psum", [128, 2048], F32),
 }
-SEMAPHORES = (["lx", "zero", "diag", "qs", "qx", "hv", "hs", "qh", "sentg", "senth", "stored",
-               "relay0", "relay1", "relayh"]
+SEMAPHORES = (["lx", "zero", "diag", "qs", "qx", "hv", "hs", "qh", "sents", "sentg", "senth", "stored",
+               "relay0", "relay1", "relayh", "sq", "s3"]
               + [n + str(i) for n in ("l", "q", "g", "h", "z", "m", "c") for i in range(4)])
 
 
@@ -86,6 +86,10 @@ def plan(cores, topo):
         a, b = ro["on_chip"][:2]
         c = ro["on_chip"][-1]
         d = ro["at_mate"][0]
+        for core, to, part in ((a, r, 0), (b, r, 1), (c, near, 0), (d, fdi, 1)):
+            for kind in "qs":
+                where = (kind + "s", blk(3, part))
+                add(core, "s", ["sq"], (cores[to], "s3", off, kind, where, where))
         add(me, "g", ["q0"], to_relay(c, "relay0", off, "s", "g", fin, 0))
         add(me, "g", [], to_relay(b, "relay0", en, "q", "g", fin))
         add(me, "g", ["q1"], to_relay(a, "relay1", inn, "q", "g", fdi, part=0),
@@ -137,33 +141,42 @@ def rank_program(g, core, T, topo):
             g.remote_dma_fused(ts, local_sem=T.sem["sent" + ph])
         return total
 
+    sem, v, a, t, sy = T.sem, g.vector, g.scalar, g.tensor, g.sync
+
+    def strip():
+        v.memset(T.ones[:], 0.0).then_inc(sem.zero, 1)
+        g.wait_ge(sem.zero, 1)
+        ones = T.ones[:, 3:3 + E:4]
+        g.affine_select(ones, ones, [[-1, W]], AluOpType.not_equal, 1.0, 0, 1).then_inc(sem.diag, 1)
+
+    def make(bs, name):
+        v.wait_ge(sem.diag, 1)
+        for b in bs:
+            v.quantize_mx(T.qs[:, blk(b)], T.ss[:, blk(b)], T.ones[:, 3 - b:3 - b + E]).then_inc(sem[name], 1)
+
     rank = T.rank_of(core)
     if rank is None:
-        for ph in ("g", "h"):
-            n = send(ph)
-            if n:
-                g.wait_ge(T.sem["sent" + ph], n)
+        if any(c["core"] == core for c in calls):
+            strip()
+            make([3], "sq")
+            for ph, n in [(ph, send(ph)) for ph in "sgh"]:
+                if n:
+                    g.wait_ge(sem["sent" + ph], n)
         return
 
     ro = roles(rank, T.cores, topo)
     near, fin, fdi = ro["near"], ro["far_inner"], ro["far_direct"]
     order = [near, fdi, fin]
     leave = [fin, near, fdi] if ro["direct"] else [fin, fdi, near]
-    sem, v, a, t, sy = T.sem, g.vector, g.scalar, g.tensor, g.sync
 
     for i, c in enumerate(leave + [rank]):
         sy.dma_start(T.tb[:, E * c:E * c + E], T.b[:, E * c:E * c + E]).then_inc(sem["l%d" % i], 16)
 
-    v.memset(T.ones[:], 0.0).then_inc(sem.zero, 1)
-    g.wait_ge(sem.zero, 1)
-    diag = T.ones[:, 3:3 + E:4]
-    g.affine_select(diag, diag, [[-1, W]], AluOpType.not_equal, 1.0, 0, 1).then_inc(sem.diag, 1)
+    strip()
 
     for i, c in enumerate(leave + [rank]):
         if c == rank:
-            v.wait_ge(sem.diag, 1)
-            for b in range(4):
-                v.quantize_mx(T.qs[:, blk(b)], T.ss[:, blk(b)], T.ones[:, 3 - b:3 - b + E]).then_inc(sem.qs, 1)
+            make([0, 1, 2], "qs")
         v.wait_ge(sem["l%d" % i], 16)
         v.quantize_mx(T.qg[:, blk(c)], T.sg[:, blk(c)], T.tb[:, E * c:E * c + E]).then_inc(sem["q%d" % i], 1)
 
@@ -172,13 +185,15 @@ def rank_program(g, core, T, topo):
     sy.wait_ge(sem.sentg, n)
     sy.dma_start(T.tx[:], T.x[:]).then_inc(sem.lx, 16)
 
-    t.wait_ge(sem.qs, 4)
+    t.wait_ge(sem.qs, 3)
     t.wait_ge(sem.q3, 1)
     for i, c in enumerate([rank] + order):
         q, s = (T.qg, T.sg) if c == rank else (T.lqg, T.lsg)
         if c != rank:
             t.wait_ge(sem["g%d" % c], got["g%d" % c])
         for b in range(4):
+            if i == 0 and b == 3:
+                t.wait_ge(sem.s3, got["s3"])
             m = t.matmul_mx(T.z[:, 512 * b:512 * b + W], T.qs[:, blk(b)], T.ss[:, blk(b)], q[:, blk(c)], s[:, blk(c)],
                             i == 0, i == 3)
             if i == 3:

from concourse.bass import DstId, RemoteDMATransfer
from concourse.mybir import dt, AluOpType, ActivationFunctionType

F8, U8, BF, F32 = "float8_e4m3fn_x4", "uint8", "bfloat16", "float32"
W = 128
E = 4 * W
SCRATCH = {
    "tb": ("sbuf", [128, 4 * E], BF), "tx": ("sbuf", [128, E], BF), "ones": ("sbuf", [128, E + 8], BF),
    "th": ("sbuf", [128, E], BF), "ty": ("sbuf", [128, 4 * W], F32),
    "qg": ("sbuf", [128, 4 * W], F8), "sg": ("sbuf", [128, 4 * W], U8),
    "qs": ("sbuf", [128, 4 * W], F8), "ss": ("sbuf", [128, 4 * W], U8),
    "qx": ("sbuf", [128, W], F8), "sx": ("sbuf", [128, W], U8),
    "qh": ("sbuf", [128, W], F8), "sh": ("sbuf", [128, W], U8),
    "lqg": ("sbuf", [128, 4 * W], F8), "lsg": ("sbuf", [128, 4 * W], U8),
    "lqh": ("sbuf", [128, 4 * W], F8), "lsh": ("sbuf", [128, 4 * W], U8),
    "rqg": ("sbuf", [128, W], F8), "rsg": ("sbuf", [128, 2 * W], U8),
    "rqh": ("sbuf", [128, W], F8), "rsh": ("sbuf", [128, W], U8),
    "z": ("psum", [128, 2048], F32), "yp": ("psum", [128, 2048], F32),
}
SEMAPHORES = (["lx", "zero", "diag", "qs", "qx", "hv", "hs", "qh", "sents", "sentg", "senth", "stored",
               "relay0", "relay1", "relayh", "sq", "s3"]
              + [n + str(i) for n in ("l", "q", "g", "h", "z", "m", "c") for i in range(4)])


def engines(mask):
    return [e for e in range(mask.bit_length()) if (mask >> e) & 1]


def blk(i, part=None):
    if part is None:
        return slice(W * i, W * (i + 1))
    return slice(W * i + W // 2 * part, W * i + W // 2 * (part + 1))


def roles(r, cores, topo):
    me = cores[r]
    far = [c for c in range(4) if topo.chip(cores[c]) != topo.chip(me)]
    back = [c for c in range(4) if c not in far]
    there = topo.chip(cores[far[0]])

    def crosses(c, others):
        return all(topo.may_write(c, cores[f]) for f in others)

    def idle(fits):
        cs = [c for c in range(topo.CHIPS * topo.CORES_PER_CHIP)
              if c not in cores and fits(topo.chip(c)) and crosses(c, far)]
        return sorted(cs, key=lambda c: (topo.die(c) != topo.die(me), c))
    return dict(near=[c for c in back if c != r][0], direct=crosses(me, far),
                on_chip=idle(lambda ch: ch == topo.chip(me)),
                at_mate=idle(lambda ch: topo.same_plane(ch, topo.chip(me)) and topo.mates(ch, there)),
                far_direct=[f for f in far if crosses(cores[f], back)][0],
                far_inner=[f for f in far if not crosses(cores[f], back)][0])


def plan(cores, topo):
    calls = []
    for r, me in enumerate(cores):
        ro = roles(r, cores, topo)
        near, fin, fdi = ro["near"], ro["far_inner"], ro["far_direct"]

        def add(core, ph, needs, *items):
            calls.append(dict(core=core, ph=ph, needs=needs, items=items))

        def to_rank(c, es, kind, ph, slot=None, part=None):
            own = (kind + ph, blk(c if ph == "g" else 0, part))
            where = own if slot is None else ("r" + kind + ph, blk(slot, part))
            return (cores[c], ph + str(r), es, kind, where, ("l" + kind + ph, blk(r, part)))

        def to_relay(core, sem, es, kind, ph, tile=0, slot=0, part=None):
            return (core, sem, es, kind, (kind + ph, blk(tile, part)), ("r" + kind + ph, blk(slot, part)))

        en = engines(topo.mask(me, cores[near]))
        off = engines(topo.mask(ro["on_chip"][0], cores[fin]))
        inn = [e for e in en if e not in off]
        h0, h1 = off[:len(off) // 2], off[len(off) // 2:]
        if ro["direct"]:
            add(me, "g", ["q0"], to_rank(fin, off, "s", "g"))
            add(me, "g", [], to_rank(fin, h0, "q", "g"))
            add(me, "g", ["q1"], to_rank(near, inn, "s", "g"))
            add(me, "g", ["q2"], to_rank(fdi, h1, "s", "g"))
            add(me, "g", [], to_rank(near, inn, "q", "g"), to_rank(fdi, off, "q", "g"))
            add(me, "h", ["qh"], to_rank(fin, h0, "s", "h"), to_rank(fdi, h1, "s", "h"))
            add(me, "h", [], to_rank(near, inn, "q", "h"), to_rank(fin, h0, "q", "h"), to_rank(fdi, h1, "q", "h"))
            add(me, "h", [], to_rank(near, inn, "s", "h"))
            continue
        a, b = ro["on_chip"][:2]
        c = ro["on_chip"][-1]
        d = ro["at_mate"][0]
        for core, to, part in ((a, r, 0), (b, r, 1), (c, near, 0), (d, fdi, 1)):
            for kind in "qs":
                where = (kind + "s", blk(3, part))
                add(core, "s", ["sq"], (cores[to], "s3", off, kind, where, where))
        add(me, "g", ["q0"], to_relay(c, "relay0", off, "s", "g", fin, 0))
        add(me, "g", [], to_relay(b, "relay0", en, "q", "g", fin))
        add(me, "g", ["q1"], to_relay(a, "relay1", inn, "q", "g", fdi, part=0),
            to_relay(d, "relay1", off, "q", "g", fdi, part=1))
        add(me, "g", [], to_relay(c, "relay1", inn, "s", "g", fdi, 1))
        add(me, "g", ["q2"], to_rank(near, inn, "s", "g"))
        add(me, "g", [], to_rank(near, en, "q", "g"))
        add(c, "g", ["relay0"], to_rank(fin, off, "s", "g", 0))
        add(b, "g", ["relay0"], to_rank(fin, off, "q", "g", 0))
        add(a, "g", ["relay1"], to_rank(fdi, off, "q", "g", 0, part=0))
        add(d, "g", ["relay1"], to_rank(fdi, off, "q", "g", 0, part=1))
        add(c, "g", ["relay1"], to_rank(fdi, off, "s", "g", 1))
        add(me, "h", ["qh"], to_relay(d, "relayh", off, "q", "h"))
        add(me, "h", [], to_relay(b, "relayh", en, "q", "h"))
        add(me, "h", [], to_relay(c, "relayh", inn, "s", "h"))
        add(me, "h", [], to_rank(near, en, "s", "h"))
        add(me, "h", [], to_rank(near, inn, "q", "h"))
        add(d, "h", ["relayh"], to_rank(fdi, off, "q", "h", 0))
        add(b, "h", ["relayh"], to_rank(fin, off, "q", "h", 0))
        add(c, "h", ["relayh"], to_rank(fin, h0, "s", "h", 0), to_rank(fdi, h1, "s", "h", 0))
    return calls


def rank_program(g, core, T, topo):
    calls = plan(T.cores, topo)
    got = {}
    for c in calls:
        for dst, name, es, *_ in c["items"]:
            if dst == core:
                got[name] = got.get(name, 0) + len(es)

    def view(kind, where):
        ap = T[where[0]][:, where[1]]
        return ap.bitcast(dt.uint8) if kind == "q" else ap

    def send(ph):
        total = 0
        for c in calls:
            if c["core"] != core or c["ph"] != ph:
                continue
            for n in c["needs"]:
                g.wait_ge(T.sem[n], got.get(n, 1))
            ts = []
            for dst, name, es, kind, s, d in c["items"]:
                rid, pid, _ = topo.addr(dst)
                ts.append(RemoteDMATransfer(dst_ids=[DstId(rid=rid, pnc=pid)], dma_engine_mask=sum(1 << e for e in es),
                                            remote_sem=T.sem[name], src=view(kind, s), dst=view(kind, d)))
                total += len(es)
            g.remote_dma_fused(ts, local_sem=T.sem["sent" + ph])
        return total

    sem, v, a, t, sy = T.sem, g.vector, g.scalar, g.tensor, g.sync

    def strip():
        v.memset(T.ones[:], 0.0).then_inc(sem.zero, 1)
        g.wait_ge(sem.zero, 1)
        ones = T.ones[:, 3:3 + E:4]
        g.affine_select(ones, ones, [[-1, W]], AluOpType.not_equal, 1.0, 0, 1).then_inc(sem.diag, 1)

    def make(bs, name):
        v.wait_ge(sem.diag, 1)
        for b in bs:
            v.quantize_mx(T.qs[:, blk(b)], T.ss[:, blk(b)], T.ones[:, 3 - b:3 - b + E]).then_inc(sem[name], 1)

    rank = T.rank_of(core)
    if rank is None:
        if any(c["core"] == core for c in calls):
            strip()
            make([3], "sq")
            for ph, n in [(ph, send(ph)) for ph in "sgh"]:
                if n:
                    g.wait_ge(sem["sent" + ph], n)
        return

    ro = roles(rank, T.cores, topo)
    near, fin, fdi = ro["near"], ro["far_inner"], ro["far_direct"]
    order = [near, fdi, fin]
    leave = [fin, near, fdi] if ro["direct"] else [fin, fdi, near]

    for i, c in enumerate(leave + [rank]):
        sy.dma_start(T.tb[:, E * c:E * c + E], T.b[:, E * c:E * c + E]).then_inc(sem["l%d" % i], 16)

    strip()

    for i, c in enumerate(leave + [rank]):
        if c == rank:
            make([0, 1, 2], "qs")
        v.wait_ge(sem["l%d" % i], 16)
        v.quantize_mx(T.qg[:, blk(c)], T.sg[:, blk(c)], T.tb[:, E * c:E * c + E]).then_inc(sem["q%d" % i], 1)

    n = send("g")
    g.wait_ge(sem.sentg, n)
    sy.wait_ge(sem.sentg, n)
    sy.dma_start(T.tx[:], T.x[:]).then_inc(sem.lx, 16)

    t.wait_ge(sem.qs, 3)
    t.wait_ge(sem.q3, 1)
    for i, c in enumerate([rank] + order):
        q, s = (T.qg, T.sg) if c == rank else (T.lqg, T.lsg)
        if c != rank:
            t.wait_ge(sem["g%d" % c], got["g%d" % c])
        for b in range(4):
            if i == 0 and b == 3:
                t.wait_ge(sem.s3, got["s3"])
            m = t.matmul_mx(T.z[:, 512 * b:512 * b + W], T.qs[:, blk(b)], T.ss[:, blk(b)], q[:, blk(c)], s[:, blk(c)],
                            i == 0, i == 3)
            if i == 3:
                m.then_inc(sem["z%d" % b], 1)

    for b in range(4):
        out, z = T.th[:, b:E:4], T.z[:, 512 * b:512 * b + W]
        if b % 2 == 0:
            a.wait_ge(sem["z%d" % b], 1)
            a.activation(out, z, ActivationFunctionType.Relu, scale=0.304).then_inc(sem.hs, 1)
        else:
            v.wait_ge(sem["z%d" % b], 1)
            v.tensor_scalar(out, z, 0.0, 0.304, AluOpType.max, AluOpType.mult).then_inc(sem.hv, 1)
    v.wait_ge(sem.hs, 2)
    v.wait_ge(sem.hv, 2)
    v.quantize_mx(T.qh[:], T.sh[:], T.th[:]).then_inc(sem.qh, 1)
    v.wait_ge(sem.lx, 16)
    v.quantize_mx(T.qx[:], T.sx[:], T.tx[:]).then_inc(sem.qx, 1)

    n = send("h")

    sy.wait_ge(sem.hs, 2)
    sy.wait_ge(sem.hv, 2)
    sy.wait_ge(sem.senth, n)
    sy.dma_start(T.h[:], T.th[:]).then_inc(sem.stored, 16)

    t.wait_ge(sem.qx, 1)
    for i, c in enumerate([rank] + order):
        if c == rank:
            t.wait_ge(sem.qh, 1)
            w, ws = T.qh[:], T.sh[:]
        else:
            t.wait_ge(sem["h%d" % c], got["h%d" % c])
            w, ws = T.lqh[:, blk(c)], T.lsh[:, blk(c)]
        yp = T.yp[:, 512 * c:512 * c + W]
        t.matmul_mx(yp, w, ws, T.qx[:], T.sx[:], True, True).then_inc(sem["m%d" % c], 1)
        if i < 3:
            a.wait_ge(sem["m%d" % c], 1)
            a.activation(T.ty[:, blk(c)], yp, ActivationFunctionType.Copy).then_inc(sem["c%d" % c], 1)
        else:
            v.wait_ge(sem["m%d" % c], 1)
            v.tensor_copy(T.ty[:, blk(c)], yp).then_inc(sem["c%d" % c], 1)
        sy.wait_ge(sem["c%d" % c], 1)
        sy.dma_start(T.y[:, blk(c)], T.ty[:, blk(c)]).then_inc(sem.stored, 16)
    sy.wait_ge(sem.stored, 80)
